import numpy as np
import ml_dtypes


def mxq(x, axis, fmt="e4m3"):
    dtype, down = {"e4m3": (ml_dtypes.float8_e4m3fn, 7), "e5m2": (ml_dtypes.float8_e5m2, 14)}[fmt]
    v = np.moveaxis(np.asarray(x, np.float32).astype(ml_dtypes.bfloat16).astype(np.float64), axis, -1)
    blocks = v.reshape(v.shape[:-1] + (-1, 32))
    amax = np.abs(blocks).max(-1, keepdims=True)
    byte = np.maximum(np.where(amax > 0, np.frexp(amax)[1] - 1 + 127, 0) - down, 1)
    scale = np.exp2(byte - 127.0)
    codes = (blocks / scale).astype(np.float32).astype(dtype).astype(np.float64)
    return np.moveaxis((codes * scale).reshape(v.shape), -1, axis)


WIDE = False


def mx_kscale(k):
    if not WIDE:
        return np.ones(k)
    levels = np.array([10, -10, 5, -5, 0])
    if k % 512:
        return np.exp2(np.random.permutation(np.resize(levels, k // 32))).repeat(32)
    a = np.empty((k // 512, 16))
    for p in range(k // 512):
        a[p, :8] = np.random.permutation(np.resize(levels, 8))
        for g in range(8):
            far = levels[np.abs(levels - a[p, g]) >= 10]
            a[p, g + 8] = far[np.random.randint(len(far))]
    return np.exp2(a.ravel()).repeat(32)


def f64(x):
    return np.asarray(x).astype(np.float64)


def striped(idx):
    return np.tile(idx.reshape(-1, 16).T, (8, 1)).astype(np.uint16)


def unstriped(offs):
    return offs[:16].T.reshape(-1).astype(np.int64)


def striped8(idx):
    return np.concatenate([x.reshape(-1, 16).T for x in idx]).astype(np.uint16)


def runs(offs, k):
    lists = np.stack([offs[16 * r : 16 * r + 16].T.reshape(-1) for r in range(8)]).astype(np.int64)
    return lists[np.arange(k) % 512 // 64]


def pack_weight(w):
    k, n = w.shape
    w = f64(np.asarray(w, np.float32).astype(ml_dtypes.bfloat16)).reshape(k // 32, 32, n)
    amax = np.abs(w).max(1)
    byte = np.clip(np.where(amax > 0, np.frexp(amax)[1] - 1 + 127 - 7, 1), 1, 254)
    scaled = (w * np.exp2(127.0 - byte)[:, None, :]).reshape(k, n).astype(np.float32)
    words = np.ascontiguousarray(scaled.reshape(k // 512, 128, 4, n).transpose(0, 1, 3, 2)).astype(ml_dtypes.float8_e4m3fn).view(np.uint8)
    return words, np.ascontiguousarray(byte.astype(np.uint8).reshape(k // 512, 16, n))


def unpack_weight(words, scales):
    g, p, n, _ = words.shape
    vals = np.ascontiguousarray(words).view(ml_dtypes.float8_e4m3fn).astype(np.float64) * np.repeat(np.exp2(scales.astype(np.float64) - 127.0), 8, axis=1)[..., None]
    return vals.transpose(0, 1, 3, 2).reshape(g * 512, n)


E2M1 = np.array([0.0, 0.5, 1.0, 1.5, 2.0, 3.0, 4.0, 6.0, -0.0, -0.5, -1.0, -1.5, -2.0, -3.0, -4.0, -6.0])


def pack_fp4(w):
    k, n = w.shape
    w = f64(np.asarray(w, np.float32).astype(ml_dtypes.bfloat16)).reshape(k // 32, 32, n)
    amax = np.abs(w).max(1)
    mant, ex = np.frexp(amax / 6.0)
    byte = np.clip(np.where(amax > 0, np.where(mant > 0.5, ex, ex - 1) + 127, 1), 1, 254)
    scaled = (w * np.exp2(127.0 - byte)[:, None, :]).reshape(k, n).astype(np.float32)
    c = np.ascontiguousarray(scaled.reshape(k // 512, 128, 4, n).transpose(0, 1, 3, 2)).astype(ml_dtypes.float4_e2m1fn).view(np.uint8) & 0xF
    words = (c[..., 0::2] | (c[..., 1::2] << 4)).reshape(k // 512, 128, 2 * n)
    return np.ascontiguousarray(words), np.ascontiguousarray(byte.astype(np.uint8).reshape(k // 512, 16, n))


def unpack_fp4(words, scales):
    g, _, n = scales.shape
    words = np.ascontiguousarray(words).reshape(g, 128, n, 2)
    nib = np.empty((g, 128, n, 4), np.uint8)
    nib[..., 0::2] = words & 0xF
    nib[..., 1::2] = words >> 4
    vals = E2M1[nib] * np.repeat(np.exp2(scales.astype(np.float64) - 127.0), 8, axis=1)[..., None]
    return vals.transpose(0, 1, 3, 2).reshape(g * 512, n)


K, T, S, H, G, W = 512, 2048, 256, 512, 2048, 128


def setup_inputs():
    n = np.random.standard_normal
    s = mx_kscale(K)[:, None]
    packed_xT = pack_weight(n((K, T)) * s)
    packed_w1 = pack_fp4(n((K, H)) / np.sqrt(K) / s)
    packed_dT = pack_weight(n((K, G)) / s)
    perm = np.random.permutation(S)
    return {
        "x_words": packed_xT[0],
        "x_scales": packed_xT[1],
        "w1_words": packed_w1[0],
        "w1_scales": packed_w1[1],
        "gs": (np.random.uniform(0.5, 1.5, (K, 1)) * s).astype(np.float32),
        "d_words": packed_dT[0],
        "d_scales": packed_dT[1],
        "offs": striped8(np.random.randint(0, T, (8, S))),
        "ka": striped8(np.random.randint(0, G, (8, H))),
        "kb": striped8(np.random.randint(0, G, (8, H))),
        "n1": striped(perm[:W]),
        "n2": striped(perm[W:]),
    }


def reference(x_words, x_scales, w1_words, w1_scales, gs, d_words, d_scales, offs, ka, kb, n1, n2):
    d_ka = unpack_weight(d_words, d_scales)[np.arange(K)[:, None], runs(ka, K)]
    xq = unpack_weight(x_words, x_scales)[np.arange(K)[:, None], runs(offs, K)]
    y = unpack_fp4(w1_words, w1_scales).T @ xq
    z = f64(gs) * y
    zq = mxq(z, 0, "e4m3")
    d_kb = unpack_weight(d_words, d_scales)[np.arange(K)[:, None], runs(kb, K)]
    h = 0.0625 * (d_ka.T @ zq + d_kb.T @ zq)
    pa = h[:, unstriped(n1)]
    pb = h[:, unstriped(n2)]
    rb = np.maximum(pa, pb)
    ra = pa / (np.abs(pb) + 0.5)
    ds = np.zeros((H, S))
    ds[:, unstriped(n1)] = ra
    out = ds.copy()
    out[:, unstriped(n2)] = rb
    return out

from contextlib import ExitStack

import concourse.mybir as mybir

K, T, S, H, G, W = 512, 2048, 256, 512, 2048, 128
FLOPS = 2 * K * H * S * 3

F32 = mybir.dt.float32
BF16 = mybir.dt.bfloat16
I32 = mybir.dt.int32
U32 = mybir.dt.uint32
U16 = mybir.dt.uint16
U8 = mybir.dt.uint8
FP8X4 = mybir.dt.float8_e4m3fn_x4
FP4X4 = mybir.dt.float4_e2m1fn_x4
ALU = mybir.AluOpType
COPY = mybir.ActivationFunctionType.Copy

P = 128
PACK = 4
QUADS = 4
HALF = 256


def tile_picked_hdaqiratio_none_p_kernel(
    tc, x_words, x_scales, w1_words, w1_scales, gs, d_words, d_scales, offs, ka, kb, n1, n2, out
):
    nc = tc.nc
    with ExitStack() as ctx:
        keep = ctx.enter_context(tc.tile_pool(name="keep", bufs=1))
        psum = ctx.enter_context(tc.psum_pool(name="psum", bufs=1))

        def sb(name, shape, dtype, tag=None):
            return keep.tile(shape, dtype, name=name, tag=tag or name, align_bytes=64)

        offs_t = sb("offs_t", [P, S // 16], U16)
        ka_t = sb("ka_t", [P, H // 16], U16)
        kb_t = sb("kb_t", [P, H // 16], U16)
        n1_t = sb("n1_t", [P, W // 16], U16)
        n2_t = sb("n2_t", [P, W // 16], U16)

        x_table = sb("x_table", [P, T], I32)
        x_bytes = sb("x_bytes", [P, T], U8)
        d_bytes = sb("d_bytes", [P, G], U8)
        w_raw = sb("w_raw", [P, 2 * H], U8)
        ws_raw = sb("ws_raw", [P, H], U8)
        gain = sb("gain", [P, PACK], F32)
        x_plane = sb("x_plane", [P, S], U8)
        d_plane = [sb("d_plane0", [P, 3 * HALF], U8), sb("d_plane1", [P, HALF], U8)]

        nc.gpsimd.memset(x_bytes[:].bitcast(I32), 0)
        for tile in (ws_raw, d_bytes, d_plane[0], d_plane[1]):
            nc.vector.memset(tile[:].bitcast(I32), 0)

        def load_w_rows(queue, q):
            queue.dma_start(
                ws_raw[32 * q : 32 * q + 4, :].bitcast(I32), w1_scales[0, 4 * q : 4 * q + 4, :].bitcast(I32)
            )

        nc.sync.dma_start(offs_t[:], offs)
        nc.scalar.dma_start(x_bytes[0:P:8, :].bitcast(I32), x_scales[0].bitcast(I32))
        nc.scalar.dma_start(d_bytes[0:P:8, :].bitcast(I32), d_scales[0].bitcast(I32))
        for tile, lists in ((ka_t, ka), (kb_t, kb), (n1_t, n1), (n2_t, n2)):
            nc.sync.dma_start(tile[:], lists)
        nc.sync.dma_start(x_table[:], x_words[0].rearrange("p c r -> p (c r)").bitcast(I32))
        nc.sync.dma_start(w_raw[:].bitcast(I32), w1_words[0].bitcast(I32))
        for q in range(2):
            load_w_rows(nc.gpsimd, q)
        nc.gpsimd.dma_start(gain[:], gs.rearrange("(p t) o -> p (t o)", t=PACK))

        x_picked_bytes = sb("x_picked_bytes", [P, S], U8)
        nc.vector.tensor_copy(x_picked_bytes[:], x_bytes[:].indirect(offs_t[:]))
        nc.vector.tensor_copy(x_plane[:].bitcast(I32), x_picked_bytes[:].bitcast(I32))
        for q in range(2, QUADS):
            load_w_rows(nc.scalar, q)
        for r in range(1, 4):
            nc.sync.dma_start(x_plane[r:P:32, :].bitcast(I32), x_picked_bytes[8 * r : P : 32, :].bitcast(I32))
        d_table = sb("d_table", [P, G], I32, tag="x_bytes")
        nc.sync.dma_start(d_table[:], d_words[0].rearrange("p c r -> p (c r)").bitcast(I32))

        def place_rows(plane, picked):
            for q in range(QUADS):
                nc.sync.dma_start(
                    plane[32 * q : 32 * q + 4, :].bitcast(I32), picked[32 * q : 32 * q + 32 : 8, :].bitcast(I32)
                )

        d_early_bytes = sb("d_early_bytes", [P, 3 * HALF], U8)
        nc.vector.tensor_copy(d_early_bytes[:, 0:H], d_bytes[:].indirect(ka_t[:]))
        nc.vector.tensor_copy(d_early_bytes[:, H : H + HALF], d_bytes[:].indirect(kb_t[:, 0:16]))
        place_rows(d_plane[0], d_early_bytes)

        w_dealt = sb("w_dealt", [P, 2 * H], U8)
        ws_dealt = sb("ws_dealt", [P, H], U8)
        nc.scalar.copy(
            w_dealt[:].bitcast(U16).rearrange("p (t m) -> p t m", t=PACK),
            w_raw[:].bitcast(U16).rearrange("p (m t) -> p t m", t=PACK),
        )
        nc.gpsimd.tensor_copy(
            ws_dealt[:].rearrange("p (t m) -> p t m", t=PACK), ws_raw[:].rearrange("p (m t) -> p t m", t=PACK)
        )

        x_picked = sb("x_picked", [P, S], U32)
        nc.vector.tensor_copy(x_picked[:], x_table[:].bitcast(U32).indirect(offs_t[:]))
        d_late_bytes = sb("d_late_bytes", [P, HALF], U8, tag="x_table")
        nc.vector.tensor_copy(d_late_bytes[:], d_bytes[:].indirect(kb_t[:, 16:32]))
        place_rows(d_plane[1], d_late_bytes)

        z_bf16 = sb("z_bf16", [P, S * PACK], BF16)
        z_codes = sb("z_codes", [P, S], U32)
        z_plane = sb("z_plane", [P, S], U8)
        for j in range(2):
            cols = slice(P * j, P * (j + 1))
            y = psum.tile([P, PACK, P], F32, name=f"y{j}")
            for t in range(PACK):
                nc.tensor.matmul_mx(
                    out=y[:, t, :],
                    lhsT=w_dealt[:, 2 * P * t : 2 * P * (t + 1)].bitcast(FP4X4),
                    lhsT_scale=ws_dealt[:, P * t : P * (t + 1)],
                    rhs=x_picked[:, cols].bitcast(FP8X4),
                    rhs_scale=x_plane[:, cols],
                    start=True,
                    stop=True,
                )
            nc.vector.tensor_tensor(
                z_bf16[:, PACK * P * j : PACK * P * (j + 1)].rearrange("p (n t) -> p n t", t=PACK),
                y[:].rearrange("p t n -> p n t"),
                gain[:].unsqueeze(1).to_broadcast([P, P, PACK]),
                ALU.mult,
            )
        for j in range(2):
            cols = slice(P * j, P * (j + 1))
            nc.vector.quantize_mx(
                out=z_codes[:, cols].bitcast(FP8X4),
                scales=z_plane[:, cols],
                in_=z_bf16[:, PACK * P * j : PACK * P * (j + 1)],
            )

        held = (("x_picked", "w_dealt"), ("ws_dealt", "x_plane"))
        d_picked = [[sb(f"d_picked{u}_{a}", [P, HALF], U32, tag=held[u][a]) for a in range(2)] for u in range(2)]
        code_lists = (ka_t, kb_t)

        def pick_d_words(u):
            for a in range(2):
                nc.vector.tensor_copy(
                    d_picked[u][a][:], d_table[:].bitcast(U32).indirect(code_lists[a][:, 16 * u : 16 * (u + 1)])
                )

        def d_scale_columns(a, b):
            first = a * H + P * b
            if first < 3 * HALF:
                return d_plane[0][:, first : first + P]
            return d_plane[1][:, first - 3 * HALF : first - 3 * HALF + P]

        h = [sb(f"h{b}", [P, S], F32) for b in range(4)]
        pa = [sb(f"pa{b}", [P, W], F32) for b in range(4)]
        pb = [sb(f"pb{b}", [P, W], F32) for b in range(4)]
        ra = [sb(f"ra{b}", [P, W], F32) for b in range(4)]
        rb = [sb(f"rb{b}", [P, W], F32) for b in range(4)]
        res = [sb(f"res{b}", [P, S], F32) for b in range(4)]

        def product(b):
            u, c = divmod(b, 2)
            acc = psum.tile([P, S], F32, name=f"acc{b}")
            for a in range(2):
                nc.tensor.matmul_mx(
                    out=acc[:],
                    lhsT=d_picked[u][a][:, P * c : P * (c + 1)].bitcast(FP8X4),
                    lhsT_scale=d_scale_columns(a, b),
                    rhs=z_codes[:].bitcast(FP8X4),
                    rhs_scale=z_plane[:],
                    start=(a == 0),
                    stop=(a == 1),
                )
            if b == 0:
                nc.scalar.activation(h[b][:], acc[:], COPY, scale=0.0625)
            else:
                nc.vector.tensor_scalar(h[b][:], acc[:], 0.0625, None, ALU.mult)

        def fetch(b):
            nc.scalar.activation(pb[b][:], h[b][:].indirect(n2_t[:]), COPY)
            nc.scalar.activation(pa[b][:], h[b][:].indirect(n1_t[:]), COPY)

        def pair(b):
            size = sb(f"size{b}", [P, W], F32)
            denom = sb(f"denom{b}", [P, W], F32)
            inv = sb(f"inv{b}", [P, W], F32)
            nc.vector.scalar_tensor_tensor(size[:], pb[b][:], -1.0, pb[b][:], ALU.mult, ALU.max)
            nc.vector.tensor_tensor(rb[b][:], pa[b][:], pb[b][:], ALU.max)
            nc.vector.tensor_scalar(denom[:], size[:], 0.5, None, ALU.add)
            nc.vector.reciprocal(inv[:], denom[:])
            nc.vector.tensor_tensor(ra[b][:], pa[b][:], inv[:], ALU.mult)

        def put(b):
            nc.scalar.activation(res[b][:].indirect(n2_t[:]), rb[b][:], COPY)
            nc.scalar.activation(res[b][:].indirect(n1_t[:]), ra[b][:], COPY)
            nc.sync.dma_start(out[P * b : P * (b + 1), :], res[b][:])

        pick_d_words(0)
        product(0)
        product(1)
        pick_d_words(1)
        fetch(0)
        pair(0)
        fetch(1)
        product(2)
        product(3)
        put(0)
        pair(1)
        fetch(2)
        put(1)
        pair(2)
        fetch(3)
        put(2)
        pair(3)
        put(3)
